import numpy as np
import ml_dtypes


def mxq(x, axis, fmt="e4m3"):
    dtype, down = {"e4m3": (ml_dtypes.float8_e4m3fn, 7), "e5m2": (ml_dtypes.float8_e5m2, 14)}[fmt]
    v = np.moveaxis(np.asarray(x, np.float32).astype(ml_dtypes.bfloat16).astype(np.float64), axis, -1)
    blocks = v.reshape(v.shape[:-1] + (-1, 32))
    amax = np.abs(blocks).max(-1, keepdims=True)
    byte = np.maximum(np.where(amax > 0, np.frexp(amax)[1] - 1 + 127, 0) - down, 1)
    scale = np.exp2(byte - 127.0)
    codes = (blocks / scale).astype(np.float32).astype(dtype).astype(np.float64)
    return np.moveaxis((codes * scale).reshape(v.shape), -1, axis)


WIDE = False


def mx_kscale(k):
    if not WIDE:
        return np.ones(k)
    levels = np.array([30, -30])
    if k % 512:
        return np.exp2(np.random.permutation(np.resize(levels, k // 32))).repeat(32)
    a = np.empty((k // 512, 16))
    for p in range(k // 512):
        a[p, :8] = np.random.permutation(np.resize(levels, 8))
        for g in range(8):
            far = levels[np.abs(levels - a[p, g]) >= 10]
            a[p, g + 8] = far[np.random.randint(len(far))]
    return np.exp2(a.ravel()).repeat(32)


def f64(x):
    return np.asarray(x).astype(np.float64)


def striped(idx):
    return np.tile(np.asarray(idx).reshape(-1, 16).T, (8, 1)).astype(np.uint16)


def unstriped(offs):
    return offs[:16].T.reshape(-1).astype(np.int64)


E2M1 = np.array([0.0, 0.5, 1.0, 1.5, 2.0, 3.0, 4.0, 6.0, -0.0, -0.5, -1.0, -1.5, -2.0, -3.0, -4.0, -6.0])


def pack_weight(w, fmt):
    k, n = w.shape
    w = f64(np.asarray(w, np.float32).astype(ml_dtypes.bfloat16)).reshape(k // 32, 32, n)
    amax = np.abs(w).max(1)
    if fmt == "e4m3":
        byte = np.frexp(amax)[1] - 1 + 127 - 7
    else:
        mant, ex = np.frexp(amax / 6.0)
        byte = np.where(mant > 0.5, ex, ex - 1) + 127
    byte = np.clip(np.where(amax > 0, byte, 1), 1, 254)
    scaled = (w * np.exp2(127.0 - byte)[:, None, :]).reshape(k, n).astype(np.float32)
    by_word = np.ascontiguousarray(scaled.reshape(k // 512, 128, 4, n).transpose(0, 1, 3, 2))
    if fmt == "e4m3":
        words = by_word.astype(ml_dtypes.float8_e4m3fn).view(np.uint8)
    else:
        c = by_word.astype(ml_dtypes.float4_e2m1fn).view(np.uint8) & 0xF
        words = (c[..., 0::2] | (c[..., 1::2] << 4)).reshape(k // 512, 128, 2 * n)
    return np.ascontiguousarray(words), np.ascontiguousarray(byte.astype(np.uint8).reshape(k // 512, 16, n))


def unpack_weight(words, scales, fmt):
    g, _, n = scales.shape
    words = np.ascontiguousarray(words).reshape(g, 128, n, -1)
    if fmt == "e4m3":
        vals = words.view(ml_dtypes.float8_e4m3fn).astype(np.float64)
    else:
        nib = np.empty((g, 128, n, 4), np.uint8)
        nib[..., 0::2] = words & 0xF
        nib[..., 1::2] = words >> 4
        vals = E2M1[nib]
    vals = vals * np.repeat(np.exp2(scales.astype(np.float64) - 127.0), 8, axis=1)[..., None]
    return vals.transpose(0, 1, 3, 2).reshape(g * 512, n)


K, T, Z, J, R, C, O, N, E = 512, 1024, 1024, 256, 512, 512, 256, 256, 1024


def setup_inputs():
    n = np.random.standard_normal
    idx = np.random.permutation(T)[:J]
    idx2 = np.random.permutation(Z)[:J]
    idx3 = np.random.permutation(C)[:J]
    idx4 = np.random.permutation(C)[:J]
    idx5 = np.random.permutation(C)[:O]
    idx6 = np.random.permutation(C)[:O]
    idx7 = np.random.permutation(E)[:O]
    fk = mx_kscale(K)
    fr = mx_kscale(R)
    xtp = pack_weight(n((K, T)) / fk[:, None], "e2m1")
    xop = pack_weight(n((K, Z)) / fk[:, None], "e4m3")
    wp = pack_weight(n((K, R)) * 1 / np.sqrt(K) * fk[:, None] * fr, "e4m3")
    wbp = pack_weight(n((R, N)) * 1 / np.sqrt(R) / fr[:, None], "e2m1")
    return {
        "xt_words": xtp[0],
        "xt_scales": xtp[1],
        "xo_words": xop[0],
        "xo_scales": xop[1],
        "w_words": wp[0],
        "w_scales": wp[1],
        "wb_words": wbp[0],
        "wb_scales": wbp[1],
        "offs": striped(idx),
        "offs2": striped(idx2),
        "offs3": striped(idx3),
        "offs4": striped(idx4),
        "offs5": striped(idx5),
        "offs6": striped(idx6),
        "offs7": striped(idx7),
    }


def reference(xt_words, xt_scales, xo_words, xo_scales, w_words, w_scales, wb_words, wb_scales, offs, offs2, offs3, offs4, offs5, offs6, offs7):
    idx = unstriped(offs)
    idx2 = unstriped(offs2)
    idx3 = unstriped(offs3)
    idx4 = unstriped(offs4)
    idx5 = unstriped(offs5)
    idx6 = unstriped(offs6)
    idx7 = unstriped(offs7)
    xtu = unpack_weight(xt_words, xt_scales, "e2m1")
    xou = unpack_weight(xo_words, xo_scales, "e4m3")
    wu = unpack_weight(w_words, w_scales, "e4m3")
    wbu = unpack_weight(wb_words, wb_scales, "e2m1")
    xtidxg = xtu[:, idx]
    a = wu.T @ xtidxg
    xoidx2g = xou[:, idx2]
    b = wu.T @ xoidx2g
    pw = np.zeros((R, C))
    pw[:, idx3] = a
    pv = np.zeros((R, C))
    pv[:, idx4] = b
    hid = np.abs(pw[:, idx5] - pv[:, idx6])
    hidq = mxq(hid, 0, "e5m2")
    p = wbu.T @ hidq
    y = np.zeros((N, E))
    y[:, idx7] = p
    return y

@@ -1,0 +1,237 @@
+from contextlib import ExitStack
+
+import concourse.mybir as mybir
+
+K, T, Z, J, R, C, O, N, E = 512, 1024, 1024, 256, 512, 512, 256, 256, 1024
+FLOPS = 2 * K * R * J * 2 + 2 * R * N * O
+
+F32 = mybir.dt.float32
+BF16 = mybir.dt.bfloat16
+I32 = mybir.dt.int32
+U32 = mybir.dt.uint32
+U16 = mybir.dt.uint16
+U8 = mybir.dt.uint8
+E4M3 = mybir.dt.float8_e4m3fn_x4
+E5M2 = mybir.dt.float8_e5m2_x4
+E2M1 = mybir.dt.float4_e2m1fn_x4
+ACT = mybir.ActivationFunctionType
+ALU = mybir.AluOpType
+
+P = 128
+PACK = 4
+HALF = O // 2
+
+
+def tile_list_oneforboth_twoboards_one_scattered_kernel(
+    tc, xt_words, xt_scales, xo_words, xo_scales, w_words, w_scales, wb_words, wb_scales,
+    offs, offs2, offs3, offs4, offs5, offs6, offs7, out,
+):
+    nc = tc.nc
+    with ExitStack() as ctx:
+        sb = ctx.enter_context(tc.tile_pool(name="sb", bufs=1))
+        ps = ctx.enter_context(tc.psum_pool(name="ps", bufs=1))
+
+        def tile(name, shape, dtype):
+            return sb.tile(shape, dtype, name=name, align_bytes=64)
+
+        lists = {}
+
+        def load_list(name, src):
+            lists[name] = tile(name, [P, J // 16], U16)
+            nc.sync.dma_start(lists[name][:], src)
+
+        def load_words(queue, dst, src):
+            queue.dma_start(dst[:].bitcast(I32), src.bitcast(I32))
+
+        def load_scales(queue, dst, src, q):
+            rows = src[0, 4 * q : 4 * q + 4, :].bitcast(I32)
+            queue.dma_start(
+                dst[32 * q : 32 * (q + 1), :].bitcast(I32), rows.unsqueeze(0).to_broadcast([8, 4, rows.shape[1]])
+            )
+
+        xt_w = tile("xt_w", [P, T], U16)
+        xt_s = tile("xt_s", [P, T], U8)
+        xo_w = tile("xo_w", [P, Z], U32)
+        xo_s = tile("xo_s", [P, Z], U8)
+        w_w = tile("w_w", [P, R], U32)
+        w_s = tile("w_s", [P, R], U8)
+        wb_w = tile("wb_w", [P, 2 * N], U8)
+        wb_s = tile("wb_s", [P, N], U8)
+
+        load_list("offs", offs)
+        for q in range(4):
+            load_scales(nc.scalar if q % 2 else nc.sync, xt_s, xt_scales, q)
+        load_words(nc.scalar, xt_w, xt_words[0])
+        load_words(nc.sync, w_w, w_words[0].rearrange("p n t -> p (n t)"))
+        load_scales(nc.scalar, w_s, w_scales, 0)
+        for q in range(2):
+            load_scales(nc.gpsimd, xo_s, xo_scales, q)
+        for q in range(1, 4):
+            load_scales(nc.scalar if q % 2 else nc.sync, w_s, w_scales, q)
+        load_list("offs2", offs2)
+        load_list("offs3", offs3)
+        for q in range(2, 4):
+            load_scales(nc.sync, xo_s, xo_scales, q)
+        load_words(nc.sync, xo_w, xo_words[0].rearrange("p n t -> p (n t)"))
+        load_list("offs4", offs4)
+        load_list("offs5", offs5)
+        load_list("offs6", offs6)
+        load_words(nc.sync, wb_w, wb_words[0])
+        for q in range(4):
+            load_scales(nc.sync, wb_s, wb_scales, q)
+        load_list("offs7", offs7)
+
+        pw = [tile("pw%d" % t, [P, C], F32) for t in range(PACK)]
+        pv = [tile("pv%d" % t, [P, C], F32) for t in range(PACK)]
+        page = [tile("page%d" % h, [P, E], F32) for h in range(N // P)]
+        for board in pw:
+            nc.vector.memset(board[:], 0.0)
+        for board in pv + page:
+            nc.gpsimd.memset(board[:], 0.0)
+
+        wd_w = tile("wd_w", [P, R], U32)
+        wd_s = [tile("wd_s%d" % u, [P, R // 2], U8) for u in range(2)]
+        xtg_w = tile("xtg_w", [P, J], U16)
+        xtg_s = tile("xtg_s", [P, J], U8)
+        xog_w = tile("xog_w", [P, J], U32)
+        xog_s = tile("xog_s", [P, J], U8)
+
+        def deal(engine, dst, src):
+            engine.copy(
+                out=dst[:].rearrange("p (t m) -> p m t", t=PACK), in_=src[:].rearrange("p (m t) -> p m t", t=PACK)
+            )
+
+        def deal_scales(u):
+            nc.vector.tensor_copy(
+                out=wd_s[u][:].rearrange("p (t m) -> p m t", t=2),
+                in_=w_s[:].rearrange("p (m t) -> p m t", t=PACK)[:, :, 2 * u : 2 * u + 2],
+            )
+
+        def gather(dst, src, name):
+            nc.vector.tensor_copy(out=dst[:], in_=src[:].indirect(lists[name][:]))
+
+        acc = {}
+
+        def first_product(name, t, words, scales, fmt):
+            acc[name, t] = ps.tile([P, J], F32, name="acc_%s%d" % (name, t))
+            cols = slice(P * t, P * (t + 1))
+            nc.tensor.matmul_mx(
+                out=acc[name, t][:], lhsT=wd_w[:, cols].bitcast(E4M3), lhsT_scale=wd_s[t // 2][:, P * (t % 2) : P * (t % 2 + 1)],
+                rhs=words[:].bitcast(fmt), rhs_scale=scales[:], start=True, stop=True,
+            )
+
+        def copy(engine, dst, src):
+            if engine is nc.scalar:
+                nc.scalar.activation(out=dst, in_=src, func=ACT.Copy)
+            else:
+                nc.vector.tensor_copy(out=dst, in_=src)
+
+        res = {}
+
+        def evac(engine, name, t):
+            res[name, t] = tile("res_%s%d" % (name, t), [P, J], F32)
+            copy(engine, res[name, t][:], acc[name, t][:])
+
+        def place(engine, name, t):
+            board, lst = (pw, "offs3") if name == "a" else (pv, "offs4")
+            copy(engine, board[t][:].indirect(lists[lst][:]), res[name, t][:])
+
+        seen = [tile("seen%d" % t, [P, O], F32) for t in range(PACK)]
+        diff = [tile("diff%d" % h, [P, PACK, HALF], F32) for h in range(2)]
+
+        def look_pw(t):
+            copy(nc.scalar, seen[t][:], pw[t][:].indirect(lists["offs5"][:]))
+
+        def look_pv(t, h):
+            nc.vector.tensor_tensor(
+                out=diff[h][:, t, :], in0=pv[t][:].indirect(lists["offs6"][:, 8 * h : 8 * (h + 1)]),
+                in1=seen[t][:, HALF * h : HALF * (h + 1)], op=ALU.subtract,
+            )
+
+        both = tile("both", [P, O], F32)
+
+        def look_pv_apart(t):
+            copy(nc.scalar, both[:], pv[t][:].indirect(lists["offs6"][:]))
+            for h in range(2):
+                cols = slice(HALF * h, HALF * (h + 1))
+                nc.vector.tensor_tensor(out=diff[h][:, t, :], in0=both[:, cols], in1=seen[t][:, cols], op=ALU.subtract)
+
+        hid = [tile("hid%d" % h, [P, HALF * PACK], BF16) for h in range(2)]
+        hq_w = [tile("hq_w%d" % h, [P, HALF], U32) for h in range(2)]
+        hq_s = [tile("hq_s%d" % h, [P, HALF], U8) for h in range(2)]
+
+        def magnitude(h):
+            nc.scalar.activation(
+                out=hid[h][:].rearrange("p (c i t) -> p c t i", i=4, t=PACK),
+                in_=diff[h][:].rearrange("p t (c i) -> p c t i", i=4), func=ACT.Abs,
+            )
+
+        def quantise(h):
+            nc.vector.quantize_mx(out=hq_w[h][:].bitcast(E5M2), scales=hq_s[h][:], in_=hid[h][:])
+
+        def second_product(h, g):
+            acc["p%d" % h, g] = ps.tile([P, HALF], F32, name="acc_a%d" % (2 * h + g))
+            nc.tensor.matmul_mx(
+                out=acc["p%d" % h, g][:], lhsT=wb_w[:, 2 * P * g : 2 * P * (g + 1)].bitcast(E2M1),
+                lhsT_scale=wb_s[:, P * g : P * (g + 1)],
+                rhs=hq_w[h][:].bitcast(E5M2), rhs_scale=hq_s[h][:], start=True, stop=True,
+            )
+
+        def evac_p(engine, h, g):
+            res["p%d" % h, g] = tile("res_p%d%d" % (h, g), [P, HALF], F32)
+            copy(engine, res["p%d" % h, g][:], acc["p%d" % h, g][:])
+
+        def place_p(engine, h, g):
+            copy(engine, page[g][:].indirect(lists["offs7"][:, 8 * h : 8 * (h + 1)]), res["p%d" % h, g][:])
+
+        S, V = nc.scalar, nc.vector
+        gather(xtg_s, xt_s, "offs")
+        gather(xtg_w, xt_w, "offs")
+        deal(S, wd_w, w_w)
+        deal_scales(0)
+        deal_scales(1)
+        for t in range(PACK):
+            first_product("a", t, xtg_w, xtg_s, E2M1)
+        evac(S, "a", 0)
+        evac(V, "a", 1)
+        place(S, "a", 0)
+        place(V, "a", 1)
+        gather(xog_w, xo_w, "offs2")
+        gather(xog_s, xo_s, "offs2")
+        for t in (1, 0, 3, 2):
+            first_product("b", t, xog_w, xog_s, E4M3)
+        evac(S, "a", 3)
+        evac(S, "a", 2)
+        place(V, "a", 3)
+        place(S, "a", 2)
+        look_pw(0)
+        look_pw(1)
+        look_pw(2)
+        look_pw(3)
+        evac(V, "b", 1)
+        place(V, "b", 1)
+        evac(S, "b", 3)
+        evac(S, "b", 0)
+        evac(S, "b", 2)
+        place(S, "b", 0)
+        place(V, "b", 3)
+        place(S, "b", 2)
+        for t in (1, 3):
+            for h in range(2):
+                look_pv(t, h)
+        look_pv_apart(0)
+        for h in range(2):
+            look_pv(2, h)
+            magnitude(h)
+        for h in range(2):
+            quantise(h)
+            for g in range(2):
+                second_product(h, g)
+            evac_p(S, h, 0)
+            evac_p(V, h, 1)
+            place_p(S, h, 0)
+            place_p(V, h, 1)
+        for g, queue in ((0, nc.scalar), (1, nc.sync)):
+            for c in range(2):
+                cols = slice(E // 2 * c, E // 2 * (c + 1))
+                queue.dma_start(out[P * g : P * (g + 1), cols], page[g][:, cols])

@@ -31,8 +31,8 @@ def tile_list_oneforboth_twoboards_one_scattered_kernel(
         sb = ctx.enter_context(tc.tile_pool(name="sb", bufs=1))
         ps = ctx.enter_context(tc.psum_pool(name="ps", bufs=1))
 
-        def tile(name, shape, dtype):
-            return sb.tile(shape, dtype, name=name, align_bytes=64)
+        def tile(name, shape, dtype, over=None):
+            return sb.tile(shape, dtype, name=name, tag=over or name, align_bytes=64)
 
         lists = {}
 
@@ -64,17 +64,15 @@ def tile_list_oneforboth_twoboards_one_scattered_kernel(
         load_words(nc.scalar, xt_w, xt_words[0])
         load_words(nc.sync, w_w, w_words[0].rearrange("p n t -> p (n t)"))
         load_scales(nc.scalar, w_s, w_scales, 0)
-        for q in range(2):
-            load_scales(nc.gpsimd, xo_s, xo_scales, q)
         for q in range(1, 4):
-            load_scales(nc.scalar if q % 2 else nc.sync, w_s, w_scales, q)
+            load_scales(nc.sync, w_s, w_scales, q)
         load_list("offs2", offs2)
-        load_list("offs3", offs3)
-        for q in range(2, 4):
+        for q in range(4):
             load_scales(nc.sync, xo_s, xo_scales, q)
+        load_list("offs3", offs3)
         load_words(nc.sync, xo_w, xo_words[0].rearrange("p n t -> p (n t)"))
-        load_list("offs4", offs4)
         load_list("offs5", offs5)
+        load_list("offs4", offs4)
         load_list("offs6", offs6)
         load_words(nc.sync, wb_w, wb_words[0])
         for q in range(4):
@@ -82,15 +80,12 @@ def tile_list_oneforboth_twoboards_one_scattered_kernel(
         load_list("offs7", offs7)
 
         pw = [tile("pw%d" % t, [P, C], F32) for t in range(PACK)]
-        pv = [tile("pv%d" % t, [P, C], F32) for t in range(PACK)]
-        page = [tile("page%d" % h, [P, E], F32) for h in range(N // P)]
-        for board in pw:
-            nc.vector.memset(board[:], 0.0)
-        for board in pv + page:
+        pv = {t: tile("pv%d" % t, [P, C], F32) for t in (0, 1)}
+        for board in pw + [pv[1], pv[0]]:
             nc.gpsimd.memset(board[:], 0.0)
 
         wd_w = tile("wd_w", [P, R], U32)
-        wd_s = [tile("wd_s%d" % u, [P, R // 2], U8) for u in range(2)]
+        wd_s = {lo: tile("wd_s%d" % lo, [P, 2 * P], U8) for lo in (0, 2)}
         xtg_w = tile("xtg_w", [P, J], U16)
         xtg_s = tile("xtg_s", [P, J], U8)
         xog_w = tile("xog_w", [P, J], U32)
@@ -101,10 +96,10 @@ def tile_list_oneforboth_twoboards_one_scattered_kernel(
                 out=dst[:].rearrange("p (t m) -> p m t", t=PACK), in_=src[:].rearrange("p (m t) -> p m t", t=PACK)
             )
 
-        def deal_scales(u):
+        def deal_scales(lo, hi):
             nc.vector.tensor_copy(
-                out=wd_s[u][:].rearrange("p (t m) -> p m t", t=2),
-                in_=w_s[:].rearrange("p (m t) -> p m t", t=PACK)[:, :, 2 * u : 2 * u + 2],
+                out=wd_s[lo][:].rearrange("p (t m) -> p t m", m=P),
+                in_=w_s[:].rearrange("p (m t) -> p t m", t=PACK)[:, lo:hi, :],
             )
 
         def gather(dst, src, name):
@@ -116,7 +111,7 @@ def tile_list_oneforboth_twoboards_one_scattered_kernel(
             acc[name, t] = ps.tile([P, J], F32, name="acc_%s%d" % (name, t))
             cols = slice(P * t, P * (t + 1))
             nc.tensor.matmul_mx(
-                out=acc[name, t][:], lhsT=wd_w[:, cols].bitcast(E4M3), lhsT_scale=wd_s[t // 2][:, P * (t % 2) : P * (t % 2 + 1)],
+                out=acc[name, t][:], lhsT=wd_w[:, cols].bitcast(E4M3), lhsT_scale=wd_s[t - t % 2][:, P * (t % 2) : P * (t % 2 + 1)],
                 rhs=words[:].bitcast(fmt), rhs_scale=scales[:], start=True, stop=True,
             )
 
@@ -128,109 +123,118 @@ def tile_list_oneforboth_twoboards_one_scattered_kernel(
 
         res = {}
 
-        def evac(engine, name, t):
-            res[name, t] = tile("res_%s%d" % (name, t), [P, J], F32)
+        page = []
+
+        def clear_page(over):
+            page.append(tile("page%d" % len(page), [P, E], F32, over))
+            nc.gpsimd.memset(page[-1][:], 0.0)
+
+        def clear_pv(t, over):
+            pv[t] = tile("pv%d" % t, [P, C], F32, over)
+            nc.gpsimd.memset(pv[t][:], 0.0)
+
+        def evac(engine, name, t, over=None):
+            res[name, t] = tile("res_%s%d" % (name, t), [P, J], F32, over)
             copy(engine, res[name, t][:], acc[name, t][:])
 
         def place(engine, name, t):
             board, lst = (pw, "offs3") if name == "a" else (pv, "offs4")
             copy(engine, board[t][:].indirect(lists[lst][:]), res[name, t][:])
 
-        seen = [tile("seen%d" % t, [P, O], F32) for t in range(PACK)]
-        diff = [tile("diff%d" % h, [P, PACK, HALF], F32) for h in range(2)]
+        seen = {}
+        diff = tile("diff", [P, PACK, O], F32)
+        both = {}
 
-        def look_pw(t):
-            copy(nc.scalar, seen[t][:], pw[t][:].indirect(lists["offs5"][:]))
+        def look_pw(engine, t):
+            copy(engine, seen[t], pw[t][:].indirect(lists["offs5"][:]))
 
-        def look_pv(t, h):
+        def look_pv(t, lo, hi):
             nc.vector.tensor_tensor(
-                out=diff[h][:, t, :], in0=pv[t][:].indirect(lists["offs6"][:, 8 * h : 8 * (h + 1)]),
-                in1=seen[t][:, HALF * h : HALF * (h + 1)], op=ALU.subtract,
+                out=diff[:, t, lo:hi], in0=pv[t][:].indirect(lists["offs6"][:, lo // 16 : hi // 16]),
+                in1=seen[t][:, lo:hi], op=ALU.subtract,
             )
 
-        both = tile("both", [P, O], F32)
+        def look_pv_apart(t, lo, hi):
+            both[t] = tile("both%d" % t, [P, hi - lo], F32)
+            copy(nc.scalar, both[t][:], pv[t][:].indirect(lists["offs6"][:, lo // 16 : hi // 16]))
+            nc.vector.tensor_tensor(out=diff[:, t, lo:hi], in0=both[t][:], in1=seen[t][:, lo:hi], op=ALU.subtract)
 
-        def look_pv_apart(t):
-            copy(nc.scalar, both[:], pv[t][:].indirect(lists["offs6"][:]))
-            for h in range(2):
-                cols = slice(HALF * h, HALF * (h + 1))
-                nc.vector.tensor_tensor(out=diff[h][:, t, :], in0=both[:, cols], in1=seen[t][:, cols], op=ALU.subtract)
-
-        hid = [tile("hid%d" % h, [P, HALF * PACK], BF16) for h in range(2)]
+        hid = tile("hid", [P, O * PACK], BF16)
         hq_w = [tile("hq_w%d" % h, [P, HALF], U32) for h in range(2)]
         hq_s = [tile("hq_s%d" % h, [P, HALF], U8) for h in range(2)]
 
-        def magnitude(h):
+        def magnitude(lo, hi):
             nc.scalar.activation(
-                out=hid[h][:].rearrange("p (c i t) -> p c t i", i=4, t=PACK),
-                in_=diff[h][:].rearrange("p t (c i) -> p c t i", i=4), func=ACT.Abs,
+                out=hid[:].rearrange("p (c t) -> p c t", t=PACK)[:, lo:hi, :],
+                in_=diff[:, :, lo:hi].rearrange("p t c -> p c t"), func=ACT.Abs,
             )
 
         def quantise(h):
-            nc.vector.quantize_mx(out=hq_w[h][:].bitcast(E5M2), scales=hq_s[h][:], in_=hid[h][:])
+            nc.vector.quantize_mx(out=hq_w[h][:].bitcast(E5M2), scales=hq_s[h][:], in_=hid[:, PACK * HALF * h : PACK * HALF * (h + 1)])
+
 
         def second_product(h, g):
-            acc["p%d" % h, g] = ps.tile([P, HALF], F32, name="acc_a%d" % (2 * h + g))
             nc.tensor.matmul_mx(
-                out=acc["p%d" % h, g][:], lhsT=wb_w[:, 2 * P * g : 2 * P * (g + 1)].bitcast(E2M1),
+                out=acc_p[h][:] if g == 0 else acc_q[:, HALF * h : HALF * (h + 1)],
+                lhsT=wb_w[:, 2 * P * g : 2 * P * (g + 1)].bitcast(E2M1),
                 lhsT_scale=wb_s[:, P * g : P * (g + 1)],
                 rhs=hq_w[h][:].bitcast(E5M2), rhs_scale=hq_s[h][:], start=True, stop=True,
             )
 
-        def evac_p(engine, h, g):
-            res["p%d" % h, g] = tile("res_p%d%d" % (h, g), [P, HALF], F32)
-            copy(engine, res["p%d" % h, g][:], acc["p%d" % h, g][:])
-
-        def place_p(engine, h, g):
-            copy(engine, page[g][:].indirect(lists["offs7"][:, 8 * h : 8 * (h + 1)]), res["p%d" % h, g][:])
+        res_p = [tile("res_p%d" % h, [P, HALF], F32) for h in range(2)]
+        res_q = tile("res_q", [P, O], F32)
 
         S, V = nc.scalar, nc.vector
         gather(xtg_s, xt_s, "offs")
         gather(xtg_w, xt_w, "offs")
         deal(S, wd_w, w_w)
-        deal_scales(0)
-        deal_scales(1)
-        for t in range(PACK):
-            first_product("a", t, xtg_w, xtg_s, E2M1)
-        evac(S, "a", 0)
-        evac(V, "a", 1)
-        place(S, "a", 0)
-        place(V, "a", 1)
-        gather(xog_w, xo_w, "offs2")
+        deal_scales(0, 2)
+        deal_scales(2, 4)
+        clear_pv(3, "w_s")
         gather(xog_s, xo_s, "offs2")
+        clear_pv(2, "xo_s")
         for t in (1, 0, 3, 2):
-            first_product("b", t, xog_w, xog_s, E4M3)
-        evac(S, "a", 3)
-        evac(S, "a", 2)
+            first_product("a", t, xtg_w, xtg_s, E2M1)
+        evac(V, "a", 1)
+        for t in (0, 3, 2):
+            evac(S, "a", t)
+        place(V, "a", 1)
+        clear_page("res_a1")
+        place(S, "a", 0)
+        clear_page("res_a0")
         place(V, "a", 3)
         place(S, "a", 2)
-        look_pw(0)
-        look_pw(1)
-        look_pw(2)
-        look_pw(3)
-        evac(V, "b", 1)
+        gather(xog_w, xo_w, "offs2")
+        for t in (1, 3, 0, 2):
+            first_product("b", t, xog_w, xog_s, E4M3)
+        seen_even = tile("seen_even", [P, 2, O], F32)
+        seen_odd = tile("seen_odd", [P, 2, O], F32, "xo_w")
+        for t in range(PACK):
+            seen[t] = (seen_odd if t % 2 else seen_even)[:, t // 2, :]
+            look_pw(V if t % 2 else S, t)
+        for t in (1, 3, 0, 2):
+            evac(S, "b", t)
         place(V, "b", 1)
-        evac(S, "b", 3)
-        evac(S, "b", 0)
-        evac(S, "b", 2)
         place(S, "b", 0)
         place(V, "b", 3)
+        look_pv(1, 0, HALF)
+        look_pv_apart(1, HALF, O)
+        look_pv(3, 0, O)
+        look_pv_apart(0, 0, O)
         place(S, "b", 2)
-        for t in (1, 3):
-            for h in range(2):
-                look_pv(t, h)
-        look_pv_apart(0)
         for h in range(2):
-            look_pv(2, h)
-            magnitude(h)
+            look_pv(2, HALF * h, HALF * (h + 1))
+            magnitude(HALF * h, HALF * (h + 1))
+        acc_p = [ps.tile([P, HALF], F32, name="acc_a%d" % h) for h in range(2)]
+        acc_q = ps.tile([P, O], F32, name="acc_a2")
         for h in range(2):
             quantise(h)
             for g in range(2):
                 second_product(h, g)
-            evac_p(S, h, 0)
-            evac_p(V, h, 1)
-            place_p(S, h, 0)
-            place_p(V, h, 1)
+            copy(V if h else S, res_p[h][:], acc_p[h][:])
+            copy(S, page[0][:].indirect(lists["offs7"][:, 8 * h : 8 * (h + 1)]), res_p[h][:])
+        copy(V, res_q[:], acc_q[:])
+        copy(V, page[1][:].indirect(lists["offs7"][:]), res_q[:])
         for g, queue in ((0, nc.scalar), (1, nc.sync)):
             for c in range(2):
                 cols = slice(E // 2 * c, E // 2 * (c + 1))

@@ -19,7 +19,11 @@ ALU = mybir.AluOpType
 
 P = 128
 PACK = 4
+QUADS = 4
+ENTRIES = 16
 HALF = O // 2
+SLICE_ORDER_A = (1, 0, 3, 2)
+SLICE_ORDER_B = (1, 3, 0, 2)
 
 
 def tile_list_oneforboth_twoboards_one_scattered_kernel(
@@ -34,19 +38,28 @@ def tile_list_oneforboth_twoboards_one_scattered_kernel(
         def tile(name, shape, dtype, over=None):
             return sb.tile(shape, dtype, name=name, tag=over or name, align_bytes=64)
 
-        lists = {}
+        def owner(t):
+            return nc.vector if t % 2 else nc.scalar
+
+        def copy(engine, dst, src):
+            if engine is nc.scalar:
+                nc.scalar.activation(out=dst, in_=src, func=ACT.Copy)
+            else:
+                nc.vector.tensor_copy(out=dst, in_=src)
 
         def load_list(name, src):
-            lists[name] = tile(name, [P, J // 16], U16)
-            nc.sync.dma_start(lists[name][:], src)
+            entries = tile(name, [P, J // ENTRIES], U16)
+            nc.sync.dma_start(entries[:], src)
+            return entries
 
         def load_words(queue, dst, src):
             queue.dma_start(dst[:].bitcast(I32), src.bitcast(I32))
 
-        def load_scales(queue, dst, src, q):
-            rows = src[0, 4 * q : 4 * q + 4, :].bitcast(I32)
+        def load_scales(queue, dst, src, quad):
+            rows = src[0, 4 * quad : 4 * quad + 4, :].bitcast(I32)
             queue.dma_start(
-                dst[32 * q : 32 * (q + 1), :].bitcast(I32), rows.unsqueeze(0).to_broadcast([8, 4, rows.shape[1]])
+                dst[32 * quad : 32 * (quad + 1), :].bitcast(I32),
+                rows.unsqueeze(0).to_broadcast([8, 4, rows.shape[1]]),
             )
 
         xt_w = tile("xt_w", [P, T], U16)
@@ -58,184 +71,136 @@ def tile_list_oneforboth_twoboards_one_scattered_kernel(
         wb_w = tile("wb_w", [P, 2 * N], U8)
         wb_s = tile("wb_s", [P, N], U8)
 
-        load_list("offs", offs)
-        for q in range(4):
-            load_scales(nc.scalar if q % 2 else nc.sync, xt_s, xt_scales, q)
+        idx = load_list("idx", offs)
+        for quad in range(QUADS):
+            load_scales(nc.scalar if quad % 2 else nc.sync, xt_s, xt_scales, quad)
         load_words(nc.scalar, xt_w, xt_words[0])
         load_words(nc.sync, w_w, w_words[0].rearrange("p n t -> p (n t)"))
-        load_scales(nc.scalar, w_s, w_scales, 0)
-        for q in range(1, 4):
-            load_scales(nc.sync, w_s, w_scales, q)
-        load_list("offs2", offs2)
-        for q in range(4):
-            load_scales(nc.sync, xo_s, xo_scales, q)
-        load_list("offs3", offs3)
+        for quad in range(QUADS):
+            load_scales(nc.sync if quad else nc.scalar, w_s, w_scales, quad)
+        idx2 = load_list("idx2", offs2)
+        for quad in range(QUADS):
+            load_scales(nc.sync, xo_s, xo_scales, quad)
+        idx3 = load_list("idx3", offs3)
         load_words(nc.sync, xo_w, xo_words[0].rearrange("p n t -> p (n t)"))
-        load_list("offs5", offs5)
-        load_list("offs4", offs4)
-        load_list("offs6", offs6)
+        idx5 = load_list("idx5", offs5)
+        idx4 = load_list("idx4", offs4)
+        idx6 = load_list("idx6", offs6)
         load_words(nc.sync, wb_w, wb_words[0])
-        for q in range(4):
-            load_scales(nc.sync, wb_s, wb_scales, q)
-        load_list("offs7", offs7)
+        for quad in range(QUADS):
+            load_scales(nc.sync, wb_s, wb_scales, quad)
+        idx7 = load_list("idx7", offs7)
 
-        pw = [tile("pw%d" % t, [P, C], F32) for t in range(PACK)]
-        pv = {t: tile("pv%d" % t, [P, C], F32) for t in (0, 1)}
-        for board in pw + [pv[1], pv[0]]:
-            nc.gpsimd.memset(board[:], 0.0)
+        def cleared(name, columns, over=None):
+            zeros = tile(name, [P, columns], F32, over)
+            nc.gpsimd.memset(zeros[:], 0.0)
+            return zeros
 
+        pw = [cleared("pw%d" % t, C) for t in range(PACK)]
+        pv = {t: cleared("pv%d" % t, C) for t in (1, 0)}
+
+        def gathered(name, dtype, src, entries):
+            picked = tile(name, [P, J], dtype)
+            nc.vector.tensor_copy(out=picked[:], in_=src[:].indirect(entries[:]))
+            return picked
+
+        xtg_s = gathered("xtg_s", U8, xt_s, idx)
+        xtg_w = gathered("xtg_w", U16, xt_w, idx)
         wd_w = tile("wd_w", [P, R], U32)
-        wd_s = {lo: tile("wd_s%d" % lo, [P, 2 * P], U8) for lo in (0, 2)}
-        xtg_w = tile("xtg_w", [P, J], U16)
-        xtg_s = tile("xtg_s", [P, J], U8)
-        xog_w = tile("xog_w", [P, J], U32)
-        xog_s = tile("xog_s", [P, J], U8)
-
-        def deal(engine, dst, src):
-            engine.copy(
-                out=dst[:].rearrange("p (t m) -> p m t", t=PACK), in_=src[:].rearrange("p (m t) -> p m t", t=PACK)
-            )
-
-        def deal_scales(lo, hi):
+        nc.scalar.copy(
+            out=wd_w[:].rearrange("p (t m) -> p m t", t=PACK), in_=w_w[:].rearrange("p (m t) -> p m t", t=PACK)
+        )
+        wd_s = [tile("wd_s%d" % u, [P, 2 * P], U8) for u in range(2)]
+        for u in range(2):
             nc.vector.tensor_copy(
-                out=wd_s[lo][:].rearrange("p (t m) -> p t m", m=P),
-                in_=w_s[:].rearrange("p (m t) -> p t m", t=PACK)[:, lo:hi, :],
+                out=wd_s[u][:].rearrange("p (t m) -> p t m", m=P),
+                in_=w_s[:].rearrange("p (m t) -> p t m", t=PACK)[:, 2 * u : 2 * u + 2, :],
             )
-
-        def gather(dst, src, name):
-            nc.vector.tensor_copy(out=dst[:], in_=src[:].indirect(lists[name][:]))
-
-        acc = {}
+        pv[3] = cleared("pv3", C, over="w_s")
+        xog_s = gathered("xog_s", U8, xo_s, idx2)
+        pv[2] = cleared("pv2", C, over="xo_s")
 
         def first_product(name, t, words, scales, fmt):
-            acc[name, t] = ps.tile([P, J], F32, name="acc_%s%d" % (name, t))
-            cols = slice(P * t, P * (t + 1))
+            bank = ps.tile([P, J], F32, name="bank_%s%d" % (name, t))
             nc.tensor.matmul_mx(
-                out=acc[name, t][:], lhsT=wd_w[:, cols].bitcast(E4M3), lhsT_scale=wd_s[t - t % 2][:, P * (t % 2) : P * (t % 2 + 1)],
+                out=bank[:], lhsT=wd_w[:, P * t : P * (t + 1)].bitcast(E4M3),
+                lhsT_scale=wd_s[t // 2][:, P * (t % 2) : P * (t % 2 + 1)],
                 rhs=words[:].bitcast(fmt), rhs_scale=scales[:], start=True, stop=True,
             )
+            return bank
 
-        def copy(engine, dst, src):
-            if engine is nc.scalar:
-                nc.scalar.activation(out=dst, in_=src, func=ACT.Copy)
-            else:
-                nc.vector.tensor_copy(out=dst, in_=src)
+        def out_of_psum(engine, name, bank):
+            values = tile(name, [P, bank.shape[1]], F32)
+            copy(engine, values[:], bank[:])
+            return values
 
-        res = {}
-
+        a_banks = {t: first_product("a", t, xtg_w, xtg_s, E2M1) for t in SLICE_ORDER_A}
+        a = {t: out_of_psum(nc.scalar, "a%d" % t, a_banks[t]) for t in SLICE_ORDER_A}
         page = []
+        for t in SLICE_ORDER_A:
+            copy(owner(t), pw[t][:].indirect(idx3[:]), a[t][:])
+            if len(page) < N // P:
+                page.append(cleared("page%d" % len(page), E, over="a%d" % t))
 
-        def clear_page(over):
-            page.append(tile("page%d" % len(page), [P, E], F32, over))
-            nc.gpsimd.memset(page[-1][:], 0.0)
-
-        def clear_pv(t, over):
-            pv[t] = tile("pv%d" % t, [P, C], F32, over)
-            nc.gpsimd.memset(pv[t][:], 0.0)
-
-        def evac(engine, name, t, over=None):
-            res[name, t] = tile("res_%s%d" % (name, t), [P, J], F32, over)
-            copy(engine, res[name, t][:], acc[name, t][:])
-
-        def place(engine, name, t):
-            board, lst = (pw, "offs3") if name == "a" else (pv, "offs4")
-            copy(engine, board[t][:].indirect(lists[lst][:]), res[name, t][:])
-
-        seen = {}
-        diff = tile("diff", [P, PACK, O], F32)
-        both = {}
-
-        def look_pw(engine, t):
-            copy(engine, seen[t], pw[t][:].indirect(lists["offs5"][:]))
-
-        def look_pv(t, lo, hi):
-            nc.vector.tensor_tensor(
-                out=diff[:, t, lo:hi], in0=pv[t][:].indirect(lists["offs6"][:, lo // 16 : hi // 16]),
-                in1=seen[t][:, lo:hi], op=ALU.subtract,
-            )
-
-        def look_pv_apart(t, lo, hi):
-            both[t] = tile("both%d" % t, [P, hi - lo], F32)
-            copy(nc.scalar, both[t][:], pv[t][:].indirect(lists["offs6"][:, lo // 16 : hi // 16]))
-            nc.vector.tensor_tensor(out=diff[:, t, lo:hi], in0=both[t][:], in1=seen[t][:, lo:hi], op=ALU.subtract)
-
-        hid = tile("hid", [P, O * PACK], BF16)
-        hq_w = [tile("hq_w%d" % h, [P, HALF], U32) for h in range(2)]
-        hq_s = [tile("hq_s%d" % h, [P, HALF], U8) for h in range(2)]
-
-        def magnitude(lo, hi):
-            nc.scalar.activation(
-                out=hid[:].rearrange("p (c t) -> p c t", t=PACK)[:, lo:hi, :],
-                in_=diff[:, :, lo:hi].rearrange("p t c -> p c t"), func=ACT.Abs,
-            )
-
-        def quantise(h):
-            nc.vector.quantize_mx(out=hq_w[h][:].bitcast(E5M2), scales=hq_s[h][:], in_=hid[:, PACK * HALF * h : PACK * HALF * (h + 1)])
-
-
-        def second_product(h, g):
-            nc.tensor.matmul_mx(
-                out=acc_p[h][:] if g == 0 else acc_q[:, HALF * h : HALF * (h + 1)],
-                lhsT=wb_w[:, 2 * P * g : 2 * P * (g + 1)].bitcast(E2M1),
-                lhsT_scale=wb_s[:, P * g : P * (g + 1)],
-                rhs=hq_w[h][:].bitcast(E5M2), rhs_scale=hq_s[h][:], start=True, stop=True,
-            )
-
-        res_p = [tile("res_p%d" % h, [P, HALF], F32) for h in range(2)]
-        res_q = tile("res_q", [P, O], F32)
-
-        S, V = nc.scalar, nc.vector
-        gather(xtg_s, xt_s, "offs")
-        gather(xtg_w, xt_w, "offs")
-        deal(S, wd_w, w_w)
-        deal_scales(0, 2)
-        deal_scales(2, 4)
-        clear_pv(3, "w_s")
-        gather(xog_s, xo_s, "offs2")
-        clear_pv(2, "xo_s")
-        for t in (1, 0, 3, 2):
-            first_product("a", t, xtg_w, xtg_s, E2M1)
-        evac(V, "a", 1)
-        for t in (0, 3, 2):
-            evac(S, "a", t)
-        place(V, "a", 1)
-        clear_page("res_a1")
-        place(S, "a", 0)
-        clear_page("res_a0")
-        place(V, "a", 3)
-        place(S, "a", 2)
-        gather(xog_w, xo_w, "offs2")
-        for t in (1, 3, 0, 2):
-            first_product("b", t, xog_w, xog_s, E4M3)
-        seen_even = tile("seen_even", [P, 2, O], F32)
-        seen_odd = tile("seen_odd", [P, 2, O], F32, "xo_w")
+        xog_w = gathered("xog_w", U32, xo_w, idx2)
+        b_banks = {t: first_product("b", t, xog_w, xog_s, E4M3) for t in SLICE_ORDER_B}
+        pw_reads = [tile("pw_reads%d" % u, [P, 2, O], F32) for u in range(2)]
+        pw_read = [pw_reads[t % 2][:, t // 2, :] for t in range(PACK)]
         for t in range(PACK):
-            seen[t] = (seen_odd if t % 2 else seen_even)[:, t // 2, :]
-            look_pw(V if t % 2 else S, t)
-        for t in (1, 3, 0, 2):
-            evac(S, "b", t)
-        place(V, "b", 1)
-        place(S, "b", 0)
-        place(V, "b", 3)
-        look_pv(1, 0, HALF)
-        look_pv_apart(1, HALF, O)
-        look_pv(3, 0, O)
-        look_pv_apart(0, 0, O)
-        place(S, "b", 2)
+            copy(owner(t), pw_read[t], pw[t][:].indirect(idx5[:]))
+        b = {t: out_of_psum(nc.scalar, "b%d" % t, b_banks[t]) for t in SLICE_ORDER_B}
+        for t in SLICE_ORDER_A:
+            copy(owner(t), pv[t][:].indirect(idx4[:]), b[t][:])
+
+        diff = tile("diff", [P, PACK, O], F32)
+        hid = tile("hid", [P, O * PACK], BF16)
+        halves = [slice(HALF * h, HALF * (h + 1)) for h in range(2)]
+
+        def half_list(entries, h):
+            return entries[:, HALF // ENTRIES * h : HALF // ENTRIES * (h + 1)]
+
+        def difference(t, h):
+            nc.vector.tensor_tensor(
+                out=diff[:, t, halves[h]], in0=pv[t][:].indirect(half_list(idx6, h)),
+                in1=pw_read[t][:, halves[h]], op=ALU.subtract,
+            )
+
+        def magnitude(h):
+            nc.scalar.activation(
+                out=hid[:].rearrange("p (o t) -> p o t", t=PACK)[:, halves[h], :],
+                in_=diff[:, :, halves[h]].rearrange("p t o -> p o t"), func=ACT.Abs,
+            )
+
+        for t in SLICE_ORDER_B:
+            difference(t, 0)
+        magnitude(0)
+        scalar_reads, last = SLICE_ORDER_B[:-1], SLICE_ORDER_B[-1]
+        difference(last, 1)
+        pv_reads = tile("pv_reads", [P, len(scalar_reads), HALF], F32)
+        for i, t in enumerate(scalar_reads):
+            copy(nc.scalar, pv_reads[:, i, :], pv[t][:].indirect(half_list(idx6, 1)))
+            nc.vector.tensor_tensor(
+                out=diff[:, t, halves[1]], in0=pv_reads[:, i, :], in1=pw_read[t][:, halves[1]], op=ALU.subtract
+            )
+        magnitude(1)
+
+        p0_banks = [ps.tile([P, HALF], F32, name="bank_a%d" % h) for h in range(2)]
+        p1_bank = ps.tile([P, O], F32, name="bank_a2")
         for h in range(2):
-            look_pv(2, HALF * h, HALF * (h + 1))
-            magnitude(HALF * h, HALF * (h + 1))
-        acc_p = [ps.tile([P, HALF], F32, name="acc_a%d" % h) for h in range(2)]
-        acc_q = ps.tile([P, O], F32, name="acc_a2")
-        for h in range(2):
-            quantise(h)
-            for g in range(2):
-                second_product(h, g)
-            copy(V if h else S, res_p[h][:], acc_p[h][:])
-            copy(S, page[0][:].indirect(lists["offs7"][:, 8 * h : 8 * (h + 1)]), res_p[h][:])
-        copy(V, res_q[:], acc_q[:])
-        copy(V, page[1][:].indirect(lists["offs7"][:]), res_q[:])
-        for g, queue in ((0, nc.scalar), (1, nc.sync)):
-            for c in range(2):
-                cols = slice(E // 2 * c, E // 2 * (c + 1))
-                queue.dma_start(out[P * g : P * (g + 1), cols], page[g][:, cols])
+            hq_w = tile("hq_w%d" % h, [P, HALF], U32)
+            hq_s = tile("hq_s%d" % h, [P, HALF], U8)
+            nc.vector.quantize_mx(
+                out=hq_w[:].bitcast(E5M2), scales=hq_s[:], in_=hid[:, PACK * HALF * h : PACK * HALF * (h + 1)]
+            )
+            for g, bank in enumerate((p0_banks[h][:], p1_bank[:, halves[h]])):
+                nc.tensor.matmul_mx(
+                    out=bank, lhsT=wb_w[:, 2 * P * g : 2 * P * (g + 1)].bitcast(E2M1),
+                    lhsT_scale=wb_s[:, P * g : P * (g + 1)],
+                    rhs=hq_w[:].bitcast(E5M2), rhs_scale=hq_s[:], start=True, stop=True,
+                )
+            p0 = out_of_psum(nc.vector if h else nc.scalar, "p0_%d" % h, p0_banks[h])
+            copy(nc.scalar, page[0][:].indirect(half_list(idx7, h)), p0[:])
+        p1 = out_of_psum(nc.vector, "p1", p1_bank)
+        copy(nc.vector, page[1][:].indirect(idx7[:]), p1[:])
+        for g, queue in enumerate((nc.scalar, nc.sync)):
+            queue.dma_start(out[P * g : P * (g + 1), :], page[g][:])

from contextlib import ExitStack

import concourse.mybir as mybir

K, T, Z, J, R, C, O, N, E = 512, 1024, 1024, 256, 512, 512, 256, 256, 1024
FLOPS = 2 * K * R * J * 2 + 2 * R * N * O

F32 = mybir.dt.float32
BF16 = mybir.dt.bfloat16
I32 = mybir.dt.int32
U32 = mybir.dt.uint32
U16 = mybir.dt.uint16
U8 = mybir.dt.uint8
E4M3 = mybir.dt.float8_e4m3fn_x4
E5M2 = mybir.dt.float8_e5m2_x4
E2M1 = mybir.dt.float4_e2m1fn_x4
ACT = mybir.ActivationFunctionType
ALU = mybir.AluOpType

P = 128
PACK = 4
QUADS = 4
ENTRIES = 16
HALF = O // 2
SLICE_ORDER_A = (1, 0, 3, 2)
SLICE_ORDER_B = (1, 3, 0, 2)


def tile_list_oneforboth_twoboards_one_scattered_kernel(
    tc, xt_words, xt_scales, xo_words, xo_scales, w_words, w_scales, wb_words, wb_scales,
    offs, offs2, offs3, offs4, offs5, offs6, offs7, out,
):
    nc = tc.nc
    with ExitStack() as ctx:
        sb = ctx.enter_context(tc.tile_pool(name="sb", bufs=1))
        ps = ctx.enter_context(tc.psum_pool(name="ps", bufs=1))

        def tile(name, shape, dtype, over=None):
            return sb.tile(shape, dtype, name=name, tag=over or name, align_bytes=64)

        def owner(t):
            return nc.vector if t % 2 else nc.scalar

        def copy(engine, dst, src):
            if engine is nc.scalar:
                nc.scalar.activation(out=dst, in_=src, func=ACT.Copy)
            else:
                nc.vector.tensor_copy(out=dst, in_=src)

        def load_list(name, src):
            entries = tile(name, [P, J // ENTRIES], U16)
            nc.sync.dma_start(entries[:], src)
            return entries

        def load_words(queue, dst, src):
            queue.dma_start(dst[:].bitcast(I32), src.bitcast(I32))

        def load_scales(queue, dst, src, quad):
            rows = src[0, 4 * quad : 4 * quad + 4, :].bitcast(I32)
            queue.dma_start(
                dst[32 * quad : 32 * (quad + 1), :].bitcast(I32),
                rows.unsqueeze(0).to_broadcast([8, 4, rows.shape[1]]),
            )

        xt_w = tile("xt_w", [P, T], U16)
        xt_s = tile("xt_s", [P, T], U8)
        xo_w = tile("xo_w", [P, Z], U32)
        xo_s = tile("xo_s", [P, Z], U8)
        w_w = tile("w_w", [P, R], U32)
        w_s = tile("w_s", [P, R], U8)
        wb_w = tile("wb_w", [P, 2 * N], U8)
        wb_s = tile("wb_s", [P, N], U8)

        idx = load_list("idx", offs)
        for quad in range(QUADS):
            load_scales(nc.scalar if quad % 2 else nc.sync, xt_s, xt_scales, quad)
        load_words(nc.scalar, xt_w, xt_words[0])
        load_words(nc.sync, w_w, w_words[0].rearrange("p n t -> p (n t)"))
        for quad in range(QUADS):
            load_scales(nc.sync if quad else nc.scalar, w_s, w_scales, quad)
        idx2 = load_list("idx2", offs2)
        for quad in range(QUADS):
            load_scales(nc.sync, xo_s, xo_scales, quad)
        idx3 = load_list("idx3", offs3)
        load_words(nc.sync, xo_w, xo_words[0].rearrange("p n t -> p (n t)"))
        idx5 = load_list("idx5", offs5)
        idx4 = load_list("idx4", offs4)
        idx6 = load_list("idx6", offs6)
        load_words(nc.sync, wb_w, wb_words[0])
        for quad in range(QUADS):
            load_scales(nc.sync, wb_s, wb_scales, quad)
        idx7 = load_list("idx7", offs7)

        def cleared(name, columns, over=None):
            zeros = tile(name, [P, columns], F32, over)
            nc.gpsimd.memset(zeros[:], 0.0)
            return zeros

        pw = [cleared("pw%d" % t, C) for t in range(PACK)]
        pv = {t: cleared("pv%d" % t, C) for t in (1, 0)}

        def gathered(name, dtype, src, entries):
            picked = tile(name, [P, J], dtype)
            nc.vector.tensor_copy(out=picked[:], in_=src[:].indirect(entries[:]))
            return picked

        xtg_s = gathered("xtg_s", U8, xt_s, idx)
        xtg_w = gathered("xtg_w", U16, xt_w, idx)
        wd_w = tile("wd_w", [P, R], U32)
        nc.scalar.copy(
            out=wd_w[:].rearrange("p (t m) -> p m t", t=PACK), in_=w_w[:].rearrange("p (m t) -> p m t", t=PACK)
        )
        wd_s = [tile("wd_s%d" % u, [P, 2 * P], U8) for u in range(2)]
        for u in range(2):
            nc.vector.tensor_copy(
                out=wd_s[u][:].rearrange("p (t m) -> p t m", m=P),
                in_=w_s[:].rearrange("p (m t) -> p t m", t=PACK)[:, 2 * u : 2 * u + 2, :],
            )
        pv[3] = cleared("pv3", C, over="w_s")
        xog_s = gathered("xog_s", U8, xo_s, idx2)
        pv[2] = cleared("pv2", C, over="xo_s")

        def first_product(name, t, words, scales, fmt):
            bank = ps.tile([P, J], F32, name="bank_%s%d" % (name, t))
            nc.tensor.matmul_mx(
                out=bank[:], lhsT=wd_w[:, P * t : P * (t + 1)].bitcast(E4M3),
                lhsT_scale=wd_s[t // 2][:, P * (t % 2) : P * (t % 2 + 1)],
                rhs=words[:].bitcast(fmt), rhs_scale=scales[:], start=True, stop=True,
            )
            return bank

        def out_of_psum(engine, name, bank):
            values = tile(name, [P, bank.shape[1]], F32)
            copy(engine, values[:], bank[:])
            return values

        a_banks = {t: first_product("a", t, xtg_w, xtg_s, E2M1) for t in SLICE_ORDER_A}
        a = {t: out_of_psum(nc.scalar, "a%d" % t, a_banks[t]) for t in SLICE_ORDER_A}
        page = []
        for t in SLICE_ORDER_A:
            copy(owner(t), pw[t][:].indirect(idx3[:]), a[t][:])
            if len(page) < N // P:
                page.append(cleared("page%d" % len(page), E, over="a%d" % t))

        xog_w = gathered("xog_w", U32, xo_w, idx2)
        b_banks = {t: first_product("b", t, xog_w, xog_s, E4M3) for t in SLICE_ORDER_B}
        pw_reads = [tile("pw_reads%d" % u, [P, 2, O], F32) for u in range(2)]
        pw_read = [pw_reads[t % 2][:, t // 2, :] for t in range(PACK)]
        for t in range(PACK):
            copy(owner(t), pw_read[t], pw[t][:].indirect(idx5[:]))
        b = {t: out_of_psum(nc.scalar, "b%d" % t, b_banks[t]) for t in SLICE_ORDER_B}
        for t in SLICE_ORDER_A:
            copy(owner(t), pv[t][:].indirect(idx4[:]), b[t][:])

        diff = tile("diff", [P, PACK, O], F32)
        hid = tile("hid", [P, O * PACK], BF16)
        halves = [slice(HALF * h, HALF * (h + 1)) for h in range(2)]

        def half_list(entries, h):
            return entries[:, HALF // ENTRIES * h : HALF // ENTRIES * (h + 1)]

        def difference(t, h):
            nc.vector.tensor_tensor(
                out=diff[:, t, halves[h]], in0=pv[t][:].indirect(half_list(idx6, h)),
                in1=pw_read[t][:, halves[h]], op=ALU.subtract,
            )

        def magnitude(h):
            nc.scalar.activation(
                out=hid[:].rearrange("p (o t) -> p o t", t=PACK)[:, halves[h], :],
                in_=diff[:, :, halves[h]].rearrange("p t o -> p o t"), func=ACT.Abs,
            )

        for t in SLICE_ORDER_B:
            difference(t, 0)
        magnitude(0)
        scalar_reads, last = SLICE_ORDER_B[:-1], SLICE_ORDER_B[-1]
        difference(last, 1)
        pv_reads = tile("pv_reads", [P, len(scalar_reads), HALF], F32)
        for i, t in enumerate(scalar_reads):
            copy(nc.scalar, pv_reads[:, i, :], pv[t][:].indirect(half_list(idx6, 1)))
            nc.vector.tensor_tensor(
                out=diff[:, t, halves[1]], in0=pv_reads[:, i, :], in1=pw_read[t][:, halves[1]], op=ALU.subtract
            )
        magnitude(1)

        p0_banks = [ps.tile([P, HALF], F32, name="bank_a%d" % h) for h in range(2)]
        p1_bank = ps.tile([P, O], F32, name="bank_a2")
        for h in range(2):
            hq_w = tile("hq_w%d" % h, [P, HALF], U32)
            hq_s = tile("hq_s%d" % h, [P, HALF], U8)
            nc.vector.quantize_mx(
                out=hq_w[:].bitcast(E5M2), scales=hq_s[:], in_=hid[:, PACK * HALF * h : PACK * HALF * (h + 1)]
            )
            for g, bank in enumerate((p0_banks[h][:], p1_bank[:, halves[h]])):
                nc.tensor.matmul_mx(
                    out=bank, lhsT=wb_w[:, 2 * P * g : 2 * P * (g + 1)].bitcast(E2M1),
                    lhsT_scale=wb_s[:, P * g : P * (g + 1)],
                    rhs=hq_w[:].bitcast(E5M2), rhs_scale=hq_s[:], start=True, stop=True,
                )
            p0 = out_of_psum(nc.vector if h else nc.scalar, "p0_%d" % h, p0_banks[h])
            copy(nc.scalar, page[0][:].indirect(half_list(idx7, h)), p0[:])
        p1 = out_of_psum(nc.vector, "p1", p1_bank)
        copy(nc.vector, page[1][:].indirect(idx7[:]), p1[:])
        for g, queue in enumerate((nc.scalar, nc.sync)):
            queue.dma_start(out[P * g : P * (g + 1), :], page[g][:])
